import numpy as np
import ml_dtypes


def mxq(x, axis, fmt="e4m3"):
    dtype, down = {"e4m3": (ml_dtypes.float8_e4m3fn, 7), "e5m2": (ml_dtypes.float8_e5m2, 14)}[fmt]
    v = np.moveaxis(np.asarray(x, np.float32).astype(ml_dtypes.bfloat16).astype(np.float64), axis, -1)
    blocks = v.reshape(v.shape[:-1] + (-1, 32))
    amax = np.abs(blocks).max(-1, keepdims=True)
    byte = np.maximum(np.where(amax > 0, np.frexp(amax)[1] - 1 + 127, 0) - down, 1)
    scale = np.exp2(byte - 127.0)
    codes = (blocks / scale).astype(np.float32).astype(dtype).astype(np.float64)
    return np.moveaxis((codes * scale).reshape(v.shape), -1, axis)


WIDE = False


def mx_kscale(k):
    if not WIDE:
        return np.ones(k)
    levels = np.array([10, -10, 5, -5, 0])
    if k % 512:
        return np.exp2(np.random.permutation(np.resize(levels, k // 32))).repeat(32)
    a = np.empty((k // 512, 16))
    for p in range(k // 512):
        a[p, :8] = np.random.permutation(np.resize(levels, 8))
        for g in range(8):
            far = levels[np.abs(levels - a[p, g]) >= 10]
            a[p, g + 8] = far[np.random.randint(len(far))]
    return np.exp2(a.ravel()).repeat(32)


def f64(x):
    return np.asarray(x).astype(np.float64)


def striped(idx):
    return np.tile(idx.reshape(-1, 16).T, (8, 1)).astype(np.uint16)


def unstriped(offs):
    return offs[:16].T.reshape(-1).astype(np.int64)


def pack_weight(w):
    k, n = w.shape
    w = f64(np.asarray(w, np.float32).astype(ml_dtypes.bfloat16)).reshape(k // 32, 32, n)
    amax = np.abs(w).max(1)
    byte = np.clip(np.where(amax > 0, np.frexp(amax)[1] - 1 + 127 - 7, 1), 1, 254)
    scaled = (w * np.exp2(127.0 - byte)[:, None, :]).reshape(k, n).astype(np.float32)
    words = np.ascontiguousarray(scaled.reshape(k // 512, 128, 4, n).transpose(0, 1, 3, 2)).astype(ml_dtypes.float8_e4m3fn).view(np.uint8)
    return words, np.ascontiguousarray(byte.astype(np.uint8).reshape(k // 512, 16, n))


def unpack_weight(words, scales):
    g, p, n, _ = words.shape
    vals = np.ascontiguousarray(words).view(ml_dtypes.float8_e4m3fn).astype(np.float64) * np.repeat(np.exp2(scales.astype(np.float64) - 127.0), 8, axis=1)[..., None]
    return vals.transpose(0, 1, 3, 2).reshape(g * 512, n)


def relu(v):
    return np.maximum(v, 0.0)


def sigmoid(v):
    return 1.0 / (1.0 + np.exp(-np.maximum(v, -700.0)))


K, T, S, N, V = 512, 2048, 512, 128, 256


def setup_inputs():
    n = np.random.standard_normal
    s = mx_kscale(K)[:, None]
    packed_xT = pack_weight(n((K, T)) * s)
    return {
        "x_words": packed_xT[0],
        "x_scales": packed_xT[1],
        "w1": (n((K, N)) / np.sqrt(K) / s).astype(np.float32),
        "recv": (np.random.uniform(0.6, 2.0, (N, V))).astype(np.float32),
        "offs": striped(np.random.permutation(T)[:S]),
        "pos1": striped(np.random.permutation(S)[:V]),
        "pos2": striped(np.random.permutation(S)[:V]),
        "pos3": striped(np.random.permutation(S)[:V]),
        "pos4": striped(np.random.permutation(S)[:V]),
    }


def reference(x_words, x_scales, w1, recv, offs, pos1, pos2, pos3, pos4):
    xq = unpack_weight(x_words, x_scales)[:, unstriped(offs)]
    y = mxq(f64(w1), 0, "e4m3").T @ xq
    dep = np.log(np.exp(y) + 1.0) + 0.3
    g0 = dep[:, unstriped(pos1)]
    bk0 = sigmoid(6.0 * (f64(recv) - g0))
    g1 = dep[:, unstriped(pos2)]
    bk1 = sigmoid(6.0 * (f64(recv) - g1))
    g2 = dep[:, unstriped(pos3)]
    bk2 = sigmoid(6.0 * (f64(recv) - g2))
    g3 = dep[:, unstriped(pos4)]
    bk3 = sigmoid(6.0 * (f64(recv) - g3))
    nblk = bk0 + bk1 + bk2 + bk3 + 0.1
    avg = (bk0 * g0 + bk1 * g1 + bk2 * g2 + bk3 * g3) / nblk
    pen = 0.8 * ((relu(f64(recv) - avg)) / (avg + 0.1)) + 0.15
    return (sigmoid((g0 - f64(recv)) / pen) + sigmoid((g1 - f64(recv)) / pen) + sigmoid((g2 - f64(recv)) / pen) + sigmoid((g3 - f64(recv)) / pen)) / 4

import concourse.mybir as mybir

K, T, S, N, V = 512, 2048, 512, 128, 256
FLOPS = 2 * K * N * S

F32 = mybir.dt.float32
BF16 = mybir.dt.bfloat16
I32 = mybir.dt.int32
U32 = mybir.dt.uint32
U16 = mybir.dt.uint16
U8 = mybir.dt.uint8
FP8X4 = mybir.dt.float8_e4m3fn_x4
ALU = mybir.AluOpType
ACT = mybir.ActivationFunctionType

P = 128
PACK = 4
LISTS = 4
HALF = S // 2
TINY = 2.0 ** -60
LEAN = 0.15 / 0.65


def tile_picked_ypcss_vis_p_kernel(tc, x_words, x_scales, w1, recv, offs, pos1, pos2, pos3, pos4, out):
    nc = tc.nc
    with tc.tile_pool(name="sb", bufs=1) as sb, tc.psum_pool(name="ps", bufs=1) as ps:
        offs_sb = sb.tile([P, S // 16], U16)
        w_raw = sb.tile([P, PACK, N], F32)
        scale_table = sb.tile([P, T], U8, align_bytes=64)
        word_table = sb.tile([P, T], I32, align_bytes=64)
        r = sb.tile([P, V], F32)
        pos_sb = [sb.tile([P, V // 16], U16, name="pos%d" % i) for i in range(LISTS)]

        nc.vector.memset(scale_table[:].bitcast(I32), 0)
        nc.sync.dma_start(offs_sb[:], offs)
        nc.sync.dma_start(w_raw[:], w1.rearrange("(p j) n -> p j n", j=PACK))
        for q in range(4):
            nc.sync.dma_start(scale_table[32 * q : 32 * q + 4, :].bitcast(I32), x_scales[0, 4 * q : 4 * q + 4, :].bitcast(I32))
        nc.sync.dma_start(word_table[:], x_words[0].rearrange("p n t -> p (n t)").bitcast(I32))
        nc.sync.dma_start(r[:], recv)
        for tile, pos in zip(pos_sb, (pos1, pos2, pos3, pos4)):
            nc.sync.dma_start(tile[:], pos)

        w_grouped = sb.tile([P, N, PACK], BF16, align_bytes=64)
        nc.vector.tensor_copy(
            w_grouped[:].rearrange("p (c i) t -> p c t i", i=4), w_raw[:].rearrange("p t (c i) -> p c t i", i=4)
        )
        w_codes = sb.tile([P, N], U32, align_bytes=64)
        w_scales = sb.tile([P, N], U8, align_bytes=64)
        nc.vector.quantize_mx(w_codes[:].bitcast(FP8X4), w_scales[:], w_grouped[:].rearrange("p n t -> p (n t)"))

        x_bytes = sb.tile([P, S], U8, align_bytes=64)
        nc.vector.tensor_copy(x_bytes[:], scale_table[:].indirect(offs_sb[:]))

        pieces = (slice(0, 256), slice(256, 384), slice(384, 512))
        x_codes = [sb.tile([P, HALF], U32, align_bytes=64, name="x_codes%d" % h) for h in range(2)]
        for h in range(2):
            nc.vector.tensor_copy(
                x_codes[h][:], word_table[:].bitcast(U32).indirect(offs_sb[:, h * HALF // 16 : (h + 1) * HALF // 16])
            )
        sig = sb.tile([P, S], F32)
        y = []
        for k, cols in enumerate(pieces):
            bank = ps.tile([P, 512], F32, name="y%d" % k)
            width = cols.stop - cols.start
            inside = cols.start % HALF
            nc.tensor.matmul_mx(
                bank[:, :width],
                lhsT=w_codes[:].bitcast(FP8X4),
                lhsT_scale=w_scales[:],
                rhs=x_codes[cols.start // HALF][:, inside : inside + width].bitcast(FP8X4),
                rhs_scale=x_bytes[:, cols],
                start=True,
                stop=True,
            )
            nc.scalar.activation(sig[:, cols], bank[:, :width], ACT.Sigmoid, scale=-1.0)
            y.append(bank[:, :width])

        r_shift = sb.tile([P, V], F32)
        r_front = sb.tile([P, V], F32)
        r_mass = sb.tile([P, V], F32)
        nc.vector.tensor_scalar(r_shift[:], r[:], -0.3, None, ALU.add)
        nc.vector.tensor_scalar(r_front[:], r[:], 0.6, None, ALU.mult)
        nc.vector.tensor_scalar(r_mass[:], r[:], 0.1, 3.0 * LEAN, ALU.add, ALU.mult)

        logs = sb.tile([P, S], F32)
        soft = sb.tile([P, S], F32)
        for k, cols in enumerate(pieces):
            nc.scalar.activation(logs[:, cols], sig[:, cols], ACT.Ln, bias=TINY)
            nc.vector.scalar_tensor_tensor(soft[:, cols], logs[:, cols], -1.0, y[k], ALU.mult, ALU.max)

        d = sb.tile([P, LISTS, V], F32)
        q = sb.tile([P, LISTS, V], F32)
        t = sb.tile([P, LISTS, V], F32)
        for i in range(LISTS):
            nc.vector.tensor_tensor(d[:, i, :], soft[:].indirect(pos_sb[i][:]), r_shift[:], ALU.subtract)
        nc.scalar.activation(q[:, 0:2, :], d[:, 0:2, :], ACT.Silu, scale=-6.0)
        nc.scalar.activation(t[:, 0:2, :], d[:, 0:2, :], ACT.Tanh, scale=-3.0)
        nc.scalar.activation(t[:, 2:4, :], d[:, 2:4, :], ACT.Tanh, scale=-3.0)
        nc.scalar.activation(q[:, 2, :], d[:, 2, :], ACT.Silu, scale=-6.0)
        nc.scalar.activation(q[:, 3, :], d[:, 3, :], ACT.Silu, scale=-6.0)

        def fresh(name):
            return sb.tile([P, V], F32, name=name)

        n0, n1, n2, n, t01, t23, tt = (fresh(name) for name in ("n0", "n1", "n2", "n", "t01", "t23", "tt"))
        x, bent, den, e, rs, a, w = (fresh(name) for name in ("x", "bent", "den", "e", "rs", "a", "w"))
        nc.vector.tensor_tensor(n0[:], r_front[:], q[:, 0, :], ALU.add)
        nc.vector.tensor_tensor(t01[:], t[:, 0, :], t[:, 1, :], ALU.add)
        nc.vector.tensor_tensor(n1[:], n0[:], q[:, 1, :], ALU.add)
        nc.vector.tensor_tensor(t23[:], t[:, 2, :], t[:, 3, :], ALU.add)
        nc.vector.tensor_tensor(n2[:], n1[:], q[:, 2, :], ALU.add)
        nc.vector.tensor_tensor(tt[:], t01[:], t23[:], ALU.add)
        nc.vector.tensor_tensor(n[:], n2[:], q[:, 3, :], ALU.add)
        nc.vector.scalar_tensor_tensor(x[:], tt[:], 4.2, r_mass[:], ALU.add, ALU.mult)
        halves = (slice(0, V // 2), slice(V // 2, V))
        for c in halves:
            nc.vector.scalar_tensor_tensor(bent[:, c], n[:, c], -LEAN, n[:, c], ALU.mult, ALU.max)
        for c in halves:
            nc.vector.tensor_tensor(e[:, c], bent[:, c], x[:, c], ALU.add)
            nc.scalar.activation(rs[:, c], e[:, c], ACT.Abs_reciprocal_sqrt)
        nc.vector.scalar_tensor_tensor(den[:], n[:], -LEAN, x[:], ALU.mult, ALU.add)
        for c in halves:
            nc.vector.tensor_tensor(a[:, c], den[:, c], rs[:, c], ALU.mult)
        for c in halves:
            nc.vector.tensor_tensor(w[:, c], a[:, c], rs[:, c], ALU.mult)

        z = sb.tile([P, LISTS, V], F32)
        sg = sb.tile([P, LISTS, V], F32)
        for i in range(LISTS):
            nc.vector.tensor_tensor(z[:, i, :], d[:, i, :], w[:], ALU.mult)
            nc.scalar.activation(sg[:, i, :], z[:, i, :], ACT.Sigmoid, scale=1.0 / 0.15)
        u, uq, v, res = (fresh(name) for name in ("u", "uq", "v", "res"))
        nc.vector.tensor_tensor(u[:], sg[:, 0, :], sg[:, 1, :], ALU.add)
        nc.vector.tensor_scalar(uq[:], u[:], 0.25, None, ALU.mult)
        for c in halves:
            nc.vector.tensor_tensor(v[:, c], sg[:, 2, c], sg[:, 3, c], ALU.add)
        for c, queue in zip(halves, (nc.sync, nc.scalar)):
            nc.vector.scalar_tensor_tensor(res[:, c], v[:, c], 0.25, uq[:, c], ALU.mult, ALU.add)
            queue.dma_start(out[:, c], res[:, c])
